import numpy as np
import ml_dtypes


def mxq(x, axis, fmt="e4m3"):
    dtype, down = {"e4m3": (ml_dtypes.float8_e4m3fn, 7), "e5m2": (ml_dtypes.float8_e5m2, 14)}[fmt]
    v = np.moveaxis(np.asarray(x, np.float32).astype(ml_dtypes.bfloat16).astype(np.float64), axis, -1)
    blocks = v.reshape(v.shape[:-1] + (-1, 32))
    amax = np.abs(blocks).max(-1, keepdims=True)
    byte = np.maximum(np.where(amax > 0, np.frexp(amax)[1] - 1 + 127, 0) - down, 1)
    scale = np.exp2(byte - 127.0)
    codes = (blocks / scale).astype(np.float32).astype(dtype).astype(np.float64)
    return np.moveaxis((codes * scale).reshape(v.shape), -1, axis)


WIDE = False


def mx_kscale(k):
    if not WIDE:
        return np.ones(k)
    levels = np.array([10, -10, 5, -5, 0])
    if k % 512:
        return np.exp2(np.random.permutation(np.resize(levels, k // 32))).repeat(32)
    a = np.empty((k // 512, 16))
    for p in range(k // 512):
        a[p, :8] = np.random.permutation(np.resize(levels, 8))
        for g in range(8):
            far = levels[np.abs(levels - a[p, g]) >= 10]
            a[p, g + 8] = far[np.random.randint(len(far))]
    return np.exp2(a.ravel()).repeat(32)


def f64(x):
    return np.asarray(x).astype(np.float64)


def striped(idx):
    return np.tile(idx.reshape(-1, 16).T, (8, 1)).astype(np.uint16)


def unstriped(offs):
    return offs[:16].T.reshape(-1).astype(np.int64)


def silu(v):
    return v / (1.0 + np.exp(-np.maximum(v, -700.0)))


K, T, E, C, H, N = 1024, 512, 4, 256, 512, 512


def by_expert(wq, xq):
    return np.concatenate([wq[e].T @ xq[:, e * C:(e + 1) * C] for e in range(E)], axis=1)


def setup_inputs():
    n = np.random.standard_normal
    s = mx_kscale(K)[:, None]
    u = mx_kscale(H)
    first = np.random.permutation(np.repeat(np.arange(E), T // E))
    second = (first + 1 + np.random.permutation(np.repeat(np.arange(E - 1), -(-T // (E - 1)))[:T])) % E
    while np.bincount(second, minlength=E).max() != T // E:
        load = np.bincount(second, minlength=E); hi, lo = int(load.argmax()), int(load.argmin())
        t = np.flatnonzero((second == hi) & (first != lo))[0]; second[t] = lo
    slot_token = np.empty(E * C, np.int64); pos = np.empty((2, T), np.int64); fill = np.zeros(E, np.int64)
    place = np.stack([np.random.permutation(C) for _ in range(E)])
    for r, deal in enumerate((first, second)):
        for t in np.random.permutation(T):
            e = deal[t]; j = e * C + place[e, fill[e]]; fill[e] += 1; slot_token[j] = t; pos[r, t] = j
    g = np.random.uniform(0.2, 0.8, T)
    return {
        "xT": (n((K, T)) * s).astype(np.float32),
        "w1": (n((E, K, H)) / np.sqrt(K) / s[None] * u[None, None, :]).astype(np.float32),
        "w2": (n((E, H, N)) / np.sqrt(H) / u[None, :, None]).astype(np.float32),
        "gate": np.stack([np.tile(g, (N, 1)), np.tile(1.0 - g, (N, 1))]).astype(np.float32),
        "offs": striped(slot_token),
        "pos1": striped(pos[0]),
        "pos2": striped(pos[1]),
    }


def reference(xT, w1, w2, gate, offs, pos1, pos2):
    idx = unstriped(offs)
    xq = mxq(f64(xT)[:, idx], 0, "e4m3")
    h = silu(by_expert(mxq(f64(w1), 1, "e4m3"), xq))
    y = by_expert(mxq(f64(w2), 1, "e4m3"), mxq(h, 0, "e4m3"))
    return f64(gate[0]) * y[:, unstriped(pos1)] + f64(gate[1]) * y[:, unstriped(pos2)]

@@ -1,0 +1,238 @@
+from contextlib import ExitStack
+
+import concourse.mybir as mybir
+
+K, T, E, C, H, N = 1024, 512, 4, 256, 512, 512
+FLOPS = 2 * E * C * (K * H + H * N)
+
+F32 = mybir.dt.float32
+BF16 = mybir.dt.bfloat16
+U32 = mybir.dt.uint32
+U16 = mybir.dt.uint16
+U8 = mybir.dt.uint8
+I32 = mybir.dt.int32
+FP8X4 = mybir.dt.float8_e4m3fn_x4
+
+P = 128
+PACK = 4
+K_PASS = P * PACK
+G = K // K_PASS
+NT = N // P
+TH = T // 2
+NH = N // 2
+W1_S_M = (128, 128, 128, 128, 80, 80, 64, 64)
+X_V_TOK = 320
+W2_ENGINE = "svsv"
+GATHER_CUTS = (0, 384, 768, 1024)
+
+
+def tile_routed_moe_kernel(tc, xT, w1, w2, gate, offs, pos1, pos2, out):
+    nc = tc.nc
+    silu = mybir.ActivationFunctionType.Silu
+    mult = mybir.AluOpType.mult
+    add = mybir.AluOpType.add
+
+    def copy_on(engine, dst, src):
+        if engine == "v":
+            nc.vector.tensor_copy(out=dst, in_=src)
+        else:
+            nc.scalar.copy(out=dst, in_=src)
+
+    with ExitStack() as ctx:
+        lists = ctx.enter_context(tc.tile_pool(name="lists", bufs=1))
+        keep = ctx.enter_context(tc.tile_pool(name="keep", bufs=1))
+        rawp = ctx.enter_context(tc.tile_pool(name="rawp", bufs=1))
+        grpp = ctx.enter_context(tc.tile_pool(name="grpp", bufs=4))
+        pinp = ctx.enter_context(tc.tile_pool(name="pinp", bufs=1))
+        hgp = ctx.enter_context(tc.tile_pool(name="hgp", bufs=2))
+        outp = ctx.enter_context(tc.tile_pool(name="outp", bufs=2))
+        psum = ctx.enter_context(tc.psum_pool(name="psum", bufs=8))
+
+        offs_t = lists.tile([P, E * C // 16], U16, name="offs_t")
+        nc.sync.dma_start(offs_t[:], offs)
+
+        x_raw = []
+        for g in range(G):
+            xr = rawp.tile([P, PACK, T], F32, name="x_raw", tag="raw%d" % (6 + g), align_bytes=64)
+            nc.sync.dma_start(out=xr[:], in_=xT[g * K_PASS:(g + 1) * K_PASS, :].rearrange("(p j) t -> p j t", j=PACK))
+            x_raw.append(xr)
+
+        warm_in = keep.tile([P, 1], F32, name="warm_in")
+        warm_out = keep.tile([P, 1], F32, name="warm_out")
+        nc.vector.memset(warm_in[:], 0.0)
+        nc.scalar.activation(out=warm_out[:], in_=warm_in[:], func=silu)
+
+        w1_raw = []
+        for e in range(E):
+            for g in range(G):
+                wr = rawp.tile([P, PACK, H], F32, name="w_raw", tag="raw%d" % (e * G + g), align_bytes=64)
+                nc.sync.dma_start(out=wr[:], in_=w1[e, g * K_PASS:(g + 1) * K_PASS, :].rearrange("(p j) c -> p j c", j=PACK))
+                w1_raw.append(wr)
+
+        pos1_t = lists.tile([P, T // 16], U16, name="pos1_t")
+        nc.sync.dma_start(pos1_t[:], pos1)
+        pos2_t = lists.tile([P, T // 16], U16, name="pos2_t")
+        nc.sync.dma_start(pos2_t[:], pos2)
+
+        gate_t = {}
+        w2_raw = []
+        for e in range(E):
+            wr = keep.tile([P, PACK, N], F32, name="w2_raw%d" % e)
+            nc.sync.dma_start(out=wr[:], in_=w2[e].rearrange("(p j) c -> p j c", j=PACK))
+            w2_raw.append(wr)
+        for nt in range(NT):
+            for r in range(2):
+                gt = keep.tile([P, T], F32, name="gate%d_%d" % (r, nt))
+                nc.sync.dma_start(out=gt[:], in_=gate[r, nt * P:(nt + 1) * P, :])
+                gate_t[(r, nt)] = gt
+
+        xw, xs = [], []
+        for g in range(G):
+            w_ = keep.tile([P, T], U32, name="xw%d" % g, align_bytes=64)
+            s_ = keep.tile([P, T], U8, name="xs%d" % g, align_bytes=64)
+            nc.vector.memset(s_[:].bitcast(I32), 0)
+            xw.append(w_)
+            xs.append(s_)
+        for g in range(G):
+            xg = grpp.tile([P, T, PACK], BF16, name="x_grp", tag="grp", align_bytes=64)
+            v_tok = X_V_TOK if g == 0 else 0
+            for engine, t0, t1 in (("v", 0, v_tok), ("s", v_tok, T)):
+                if t1 == t0:
+                    continue
+                copy_on(
+                    engine,
+                    xg[:, t0:t1, :].rearrange("p (c i) j -> p c j i", i=4),
+                    x_raw[g][:, :, t0:t1].rearrange("p j (c i) -> p c j i", i=4),
+                )
+            nc.vector.quantize_mx(out=xw[g][:].bitcast(FP8X4), scales=xs[g][:], in_=xg[:].rearrange("p t j -> p (t j)"))
+
+        ysb = [keep.tile([P, E * C], F32, name="ysb%d" % nt) for nt in range(NT)]
+        xgw, xgs, w1g, w1c, w1s, banks, hgs, hc, hs = {}, {}, {}, {}, {}, {}, {}, {}, {}
+        w2g, w2c, w2s = {}, {}, {}
+
+        def gathers(k):
+            a, b = GATHER_CUTS[k], GATHER_CUTS[k + 1]
+            lst = offs_t[:, a // 16:b // 16]
+            tags = ("xgw%d" % k, "xgs%d" % k) if k < 2 else ("pin0", "pin1")
+            xgw[k] = pinp.tile([P, G, b - a], U32, name="xgw", tag=tags[0], align_bytes=64)
+            xgs[k] = pinp.tile([P, G, b - a], U8, name="xgs", tag=tags[1], align_bytes=64)
+            for g in range(G):
+                nc.vector.tensor_copy(out=xgw[k][:, g, :], in_=xw[g][:].indirect(lst))
+                nc.vector.tensor_copy(out=xgs[k][:, g, :], in_=xs[g][:].indirect(lst))
+
+        def w1_interleave(ci):
+            if ci < 2:
+                wg = pinp.tile([P, PACK, P, PACK], BF16, name="w1_grp_p", tag="pin%d" % ci, align_bytes=64)
+            else:
+                wg = grpp.tile([P, PACK, P, PACK], BF16, name="w1_grp", tag="grp", align_bytes=64)
+            dst = wg[:].rearrange("p t m j -> p m j t")
+            src = w1_raw[ci][:].rearrange("p j (m t) -> p m j t", t=PACK)
+            s_m = W1_S_M[ci]
+            copy_on("s", dst[:, 0:s_m], src[:, 0:s_m])
+            if s_m < P:
+                copy_on("v", dst[:, s_m:P], src[:, s_m:P])
+            w1g[ci] = wg
+
+        def w1_quantise(ci):
+            w1c[ci] = keep.tile([P, H], U32, name="w1c%d" % ci, align_bytes=64)
+            w1s[ci] = keep.tile([P, H], U8, name="w1s%d" % ci, align_bytes=64)
+            nc.vector.quantize_mx(out=w1c[ci][:].bitcast(FP8X4), scales=w1s[ci][:], in_=w1g[ci][:].rearrange("p t m j -> p (t m j)"))
+
+        def layer1(e):
+            for hf in range(C // P):
+                bank = psum.tile([P, PACK, P], F32, name="abank", tag="bank")
+                slot0 = e * C + hf * P
+                k = max(i for i in range(3) if GATHER_CUTS[i] <= slot0)
+                cols = slice(slot0 - GATHER_CUTS[k], slot0 - GATHER_CUTS[k] + P)
+                for t in range(PACK):
+                    m_cols = slice(t * P, (t + 1) * P)
+                    for g in range(G):
+                        nc.tensor.matmul_mx(
+                            out=bank[:, t, :],
+                            lhsT=w1c[e * G + g][:, m_cols].bitcast(FP8X4),
+                            lhsT_scale=w1s[e * G + g][:, m_cols],
+                            rhs=xgw[k][:, g, cols].bitcast(FP8X4),
+                            rhs_scale=xgs[k][:, g, cols],
+                            start=(g == 0),
+                            stop=(g == G - 1),
+                        )
+                banks[(e, hf)] = bank
+
+        def hidden(e):
+            if e < 2:
+                hg = rawp.tile([P, C, PACK], BF16, name="hgrp_r", tag="raw%d" % (2 * e + 5), align_bytes=64)
+            else:
+                hg = hgp.tile([P, C, PACK], BF16, name="hgrp", tag="hgrp", align_bytes=64)
+            for hf in range(C // P):
+                nc.scalar.activation(out=hg[:, hf * P:(hf + 1) * P, :], in_=banks[(e, hf)][:].rearrange("p t n -> p n t"), func=silu)
+            hc[e] = keep.tile([P, C], U32, name="hc%d" % e, align_bytes=64)
+            hs[e] = keep.tile([P, C], U8, name="hs%d" % e, align_bytes=64)
+            nc.vector.quantize_mx(out=hc[e][:].bitcast(FP8X4), scales=hs[e][:], in_=hg[:].rearrange("p n t -> p (n t)"))
+
+        def w2_prepare(e):
+            wg = grpp.tile([P, NT, P, PACK], BF16, name="w2_grp", tag="grp", align_bytes=64)
+            copy_on(
+                W2_ENGINE[e],
+                wg[:].rearrange("p q (c i) j -> p q c j i", i=4),
+                w2_raw[e][:].rearrange("p j (q c i) -> p q c j i", q=NT, i=4),
+            )
+            w2c[e] = keep.tile([P, NT, P], U32, name="w2c%d" % e, align_bytes=64)
+            w2s[e] = keep.tile([P, NT, P], U8, name="w2s%d" % e, align_bytes=64)
+            nc.vector.quantize_mx(
+                out=w2c[e][:].rearrange("p q c -> p (q c)").bitcast(FP8X4),
+                scales=w2s[e][:].rearrange("p q c -> p (q c)"),
+                in_=wg[:].rearrange("p q c j -> p (q c j)"),
+            )
+
+        def layer2(pair):
+            ybanks = [psum.tile([P, 2 * C], F32, name="ybank", tag="bank") for nt in range(NT)]
+            for half in range(2):
+                e = 2 * pair + half
+                for nt in range(NT):
+                    nc.tensor.matmul_mx(
+                        out=ybanks[nt][:, half * C:(half + 1) * C],
+                        lhsT=w2c[e][:, nt].bitcast(FP8X4),
+                        lhsT_scale=w2s[e][:, nt],
+                        rhs=hc[e][:].bitcast(FP8X4),
+                        rhs_scale=hs[e][:],
+                        start=True,
+                        stop=True,
+                    )
+            for nt in range(NT):
+                nc.scalar.copy(out=ysb[nt][:, pair * 2 * C:(pair + 1) * 2 * C], in_=ybanks[nt][:])
+
+        def combine(nt):
+            pr1 = outp.tile([P, T], F32, name="pr1", tag="pr1")
+            pr2 = outp.tile([P, T], F32, name="pr2", tag="pr2")
+            res = outp.tile([P, T], F32, name="res", tag="res")
+            nc.vector.tensor_tensor(pr1[:], ysb[nt][:].indirect(pos1_t[:]), gate_t[(0, nt)][:], mult)
+            nc.vector.tensor_tensor(pr2[:], ysb[nt][:].indirect(pos2_t[:]), gate_t[(1, nt)][:], mult)
+            nc.vector.tensor_tensor(res[:], pr1[:], pr2[:], add)
+            nc.sync.dma_start(out=out[nt * P:(nt + 1) * P, :], in_=res[:])
+
+        gathers(0)
+        w1_interleave(0)
+        w1_interleave(1)
+        gathers(1)
+        for e in range(E):
+            w1_quantise(2 * e)
+            w1_quantise(2 * e + 1)
+            layer1(e)
+            if e + 1 < E:
+                w1_interleave(2 * e + 2)
+                w1_interleave(2 * e + 3)
+            if e == 0:
+                gathers(2)
+            if e == 2:
+                hidden(0)
+        hidden(1)
+        w2_prepare(0)
+        w2_prepare(1)
+        layer2(0)
+        hidden(2)
+        w2_prepare(2)
+        w2_prepare(3)
+        hidden(3)
+        layer2(1)
+        for nt in range(NT):
+            combine(nt)

@@ -1,6 +1,7 @@
 from contextlib import ExitStack
 
 import concourse.mybir as mybir
+from concourse.masks import make_identity
 
 K, T, E, C, H, N = 1024, 512, 4, 256, 512, 512
 FLOPS = 2 * E * C * (K * H + H * N)
@@ -22,7 +23,7 @@ TH = T // 2
 NH = N // 2
 W1_S_M = (128, 128, 128, 128, 80, 80, 64, 64)
 X_V_TOK = 320
-W2_ENGINE = "svsv"
+W2_ENGINE = "vvvv"
 GATHER_CUTS = (0, 384, 768, 1024)
 
 
@@ -46,6 +47,7 @@ def tile_routed_moe_kernel(tc, xT, w1, w2, gate, offs, pos1, pos2, out):
         pinp = ctx.enter_context(tc.tile_pool(name="pinp", bufs=1))
         hgp = ctx.enter_context(tc.tile_pool(name="hgp", bufs=2))
         outp = ctx.enter_context(tc.tile_pool(name="outp", bufs=2))
+        resp = ctx.enter_context(tc.tile_pool(name="resp", bufs=NT))
         psum = ctx.enter_context(tc.psum_pool(name="psum", bufs=8))
 
         offs_t = lists.tile([P, E * C // 16], U16, name="offs_t")
@@ -56,6 +58,9 @@ def tile_routed_moe_kernel(tc, xT, w1, w2, gate, offs, pos1, pos2, out):
             xr = rawp.tile([P, PACK, T], F32, name="x_raw", tag="raw%d" % (6 + g), align_bytes=64)
             nc.sync.dma_start(out=xr[:], in_=xT[g * K_PASS:(g + 1) * K_PASS, :].rearrange("(p j) t -> p j t", j=PACK))
             x_raw.append(xr)
+
+        ident = keep.tile([P, P], F32, name="ident")
+        make_identity(nc, ident[:])
 
         warm_in = keep.tile([P, 1], F32, name="warm_in")
         warm_out = keep.tile([P, 1], F32, name="warm_out")
@@ -86,13 +91,12 @@ def tile_routed_moe_kernel(tc, xT, w1, w2, gate, offs, pos1, pos2, out):
                 nc.sync.dma_start(out=gt[:], in_=gate[r, nt * P:(nt + 1) * P, :])
                 gate_t[(r, nt)] = gt
 
-        xw, xs = [], []
+        xw = []
+        xs = keep.tile([P, T], U8, name="xs", align_bytes=64)
+        nc.vector.memset(xs[:].bitcast(I32), 0)
         for g in range(G):
             w_ = keep.tile([P, T], U32, name="xw%d" % g, align_bytes=64)
-            s_ = keep.tile([P, T], U8, name="xs%d" % g, align_bytes=64)
-            nc.vector.memset(s_[:].bitcast(I32), 0)
             xw.append(w_)
-            xs.append(s_)
         for g in range(G):
             xg = grpp.tile([P, T, PACK], BF16, name="x_grp", tag="grp", align_bytes=64)
             v_tok = X_V_TOK if g == 0 else 0
@@ -104,7 +108,7 @@ def tile_routed_moe_kernel(tc, xT, w1, w2, gate, offs, pos1, pos2, out):
                     xg[:, t0:t1, :].rearrange("p (c i) j -> p c j i", i=4),
                     x_raw[g][:, :, t0:t1].rearrange("p j (c i) -> p c j i", i=4),
                 )
-            nc.vector.quantize_mx(out=xw[g][:].bitcast(FP8X4), scales=xs[g][:], in_=xg[:].rearrange("p t j -> p (t j)"))
+            nc.vector.quantize_mx(out=xw[g][:].bitcast(FP8X4), scales=xs[PACK * g:P, :], in_=xg[:].rearrange("p t j -> p (t j)"))
 
         ysb = [keep.tile([P, E * C], F32, name="ysb%d" % nt) for nt in range(NT)]
         xgw, xgs, w1g, w1c, w1s, banks, hgs, hc, hs = {}, {}, {}, {}, {}, {}, {}, {}, {}
@@ -115,10 +119,10 @@ def tile_routed_moe_kernel(tc, xT, w1, w2, gate, offs, pos1, pos2, out):
             lst = offs_t[:, a // 16:b // 16]
             tags = ("xgw%d" % k, "xgs%d" % k) if k < 2 else ("pin0", "pin1")
             xgw[k] = pinp.tile([P, G, b - a], U32, name="xgw", tag=tags[0], align_bytes=64)
-            xgs[k] = pinp.tile([P, G, b - a], U8, name="xgs", tag=tags[1], align_bytes=64)
+            xgs[k] = pinp.tile([P, b - a], U8, name="xgs", tag=tags[1], align_bytes=64)
             for g in range(G):
                 nc.vector.tensor_copy(out=xgw[k][:, g, :], in_=xw[g][:].indirect(lst))
-                nc.vector.tensor_copy(out=xgs[k][:, g, :], in_=xs[g][:].indirect(lst))
+            nc.vector.tensor_copy(out=xgs[k][:], in_=xs[:].indirect(lst))
 
         def w1_interleave(ci):
             if ci < 2:
@@ -152,7 +156,7 @@ def tile_routed_moe_kernel(tc, xT, w1, w2, gate, offs, pos1, pos2, out):
                             lhsT=w1c[e * G + g][:, m_cols].bitcast(FP8X4),
                             lhsT_scale=w1s[e * G + g][:, m_cols],
                             rhs=xgw[k][:, g, cols].bitcast(FP8X4),
-                            rhs_scale=xgs[k][:, g, cols],
+                            rhs_scale=xgs[k][PACK * g:P, cols],
                             start=(g == 0),
                             stop=(g == G - 1),
                         )
@@ -204,10 +208,16 @@ def tile_routed_moe_kernel(tc, xT, w1, w2, gate, offs, pos1, pos2, out):
         def combine(nt):
             pr1 = outp.tile([P, T], F32, name="pr1", tag="pr1")
             pr2 = outp.tile([P, T], F32, name="pr2", tag="pr2")
-            res = outp.tile([P, T], F32, name="res", tag="res")
+            res = resp.tile([P, T], F32, name="res", tag="res")
             nc.vector.tensor_tensor(pr1[:], ysb[nt][:].indirect(pos1_t[:]), gate_t[(0, nt)][:], mult)
             nc.vector.tensor_tensor(pr2[:], ysb[nt][:].indirect(pos2_t[:]), gate_t[(1, nt)][:], mult)
-            nc.vector.tensor_tensor(res[:], pr1[:], pr2[:], add)
+            if nt < NT - 1:
+                acc = psum.tile([P, T], F32, name="obank", tag="bank")
+                nc.tensor.matmul(acc[:], lhsT=ident[:], rhs=pr1[:], start=True, stop=False)
+                nc.tensor.matmul(acc[:], lhsT=ident[:], rhs=pr2[:], start=False, stop=True)
+                nc.scalar.copy(out=res[:], in_=acc[:])
+            else:
+                nc.vector.tensor_tensor(res[:], pr1[:], pr2[:], add)
             nc.sync.dma_start(out=out[nt * P:(nt + 1) * P, :], in_=res[:])
 
         gathers(0)

@@ -24,6 +24,8 @@ NH = N // 2
 W1_S_M = (128, 128, 128, 128, 80, 80, 64, 64)
 X_V_TOK = 320
 W2_ENGINE = "vvvv"
+W2_BYTES = PACK * N * 4
+H_ON_W2 = (None, 0, 0, 2)
 GATHER_CUTS = (0, 384, 768, 1024)
 
 
@@ -47,6 +49,7 @@ def tile_routed_moe_kernel(tc, xT, w1, w2, gate, offs, pos1, pos2, out):
         pinp = ctx.enter_context(tc.tile_pool(name="pinp", bufs=1))
         hgp = ctx.enter_context(tc.tile_pool(name="hgp", bufs=2))
         outp = ctx.enter_context(tc.tile_pool(name="outp", bufs=2))
+        w2p = ctx.enter_context(tc.tile_pool(name="w2p", bufs=1))
         resp = ctx.enter_context(tc.tile_pool(name="resp", bufs=NT))
         psum = ctx.enter_context(tc.psum_pool(name="psum", bufs=8))
 
@@ -68,11 +71,27 @@ def tile_routed_moe_kernel(tc, xT, w1, w2, gate, offs, pos1, pos2, out):
         nc.scalar.activation(out=warm_out[:], in_=warm_in[:], func=silu)
 
         w1_raw = []
-        for e in range(E):
+        w2_raw = []
+
+        def load_w1(e):
             for g in range(G):
                 wr = rawp.tile([P, PACK, H], F32, name="w_raw", tag="raw%d" % (e * G + g), align_bytes=64)
                 nc.sync.dma_start(out=wr[:], in_=w1[e, g * K_PASS:(g + 1) * K_PASS, :].rearrange("(p j) c -> p j c", j=PACK))
                 w1_raw.append(wr)
+
+        def load_w2(e):
+            wr = w2p.tile([P, PACK, N], F32, name="w2_raw%d" % e, align_bytes=64, offset=e * W2_BYTES)
+            nc.sync.dma_start(out=wr[:], in_=w2[e].rearrange("(p j) c -> p j c", j=PACK))
+            w2_raw.append(wr)
+
+        load_w1(0)
+        load_w1(1)
+        load_w1(2)
+        load_w2(0)
+        load_w1(3)
+        load_w2(1)
+        load_w2(2)
+        load_w2(3)
 
         pos1_t = lists.tile([P, T // 16], U16, name="pos1_t")
         nc.sync.dma_start(pos1_t[:], pos1)
@@ -80,11 +99,6 @@ def tile_routed_moe_kernel(tc, xT, w1, w2, gate, offs, pos1, pos2, out):
         nc.sync.dma_start(pos2_t[:], pos2)
 
         gate_t = {}
-        w2_raw = []
-        for e in range(E):
-            wr = keep.tile([P, PACK, N], F32, name="w2_raw%d" % e)
-            nc.sync.dma_start(out=wr[:], in_=w2[e].rearrange("(p j) c -> p j c", j=PACK))
-            w2_raw.append(wr)
         for nt in range(NT):
             for r in range(2):
                 gt = keep.tile([P, T], F32, name="gate%d_%d" % (r, nt))
@@ -164,13 +178,18 @@ def tile_routed_moe_kernel(tc, xT, w1, w2, gate, offs, pos1, pos2, out):
 
         def hidden(e):
             if e < 2:
-                hg = rawp.tile([P, C, PACK], BF16, name="hgrp_r", tag="raw%d" % (2 * e + 5), align_bytes=64)
+                hg = rawp.tile([P, C, PACK], BF16, name="hgrp_r", tag="raw%d" % (e + 4), align_bytes=64)
             else:
                 hg = hgp.tile([P, C, PACK], BF16, name="hgrp", tag="hgrp", align_bytes=64)
             for hf in range(C // P):
                 nc.scalar.activation(out=hg[:, hf * P:(hf + 1) * P, :], in_=banks[(e, hf)][:].rearrange("p t n -> p n t"), func=silu)
-            hc[e] = keep.tile([P, C], U32, name="hc%d" % e, align_bytes=64)
-            hs[e] = keep.tile([P, C], U8, name="hs%d" % e, align_bytes=64)
+            if e == 0:
+                hc[e] = keep.tile([P, C], U32, name="hc%d" % e, align_bytes=64)
+                hs[e] = keep.tile([P, C], U8, name="hs%d" % e, align_bytes=64)
+            else:
+                base = H_ON_W2[e] * W2_BYTES + (e % 2) * 2 * C * 4
+                hc[e] = w2p.tile([P, C], U32, name="hc%d" % e, align_bytes=64, offset=base)
+                hs[e] = w2p.tile([P, C], U8, name="hs%d" % e, align_bytes=64, offset=base + C * 4)
             nc.vector.quantize_mx(out=hc[e][:].bitcast(FP8X4), scales=hs[e][:], in_=hg[:].rearrange("p n t -> p (n t)"))
 
         def w2_prepare(e):
@@ -224,25 +243,29 @@ def tile_routed_moe_kernel(tc, xT, w1, w2, gate, offs, pos1, pos2, out):
         w1_interleave(0)
         w1_interleave(1)
         gathers(1)
-        for e in range(E):
+        for e in range(E - 1):
             w1_quantise(2 * e)
             w1_quantise(2 * e + 1)
             layer1(e)
-            if e + 1 < E:
+            if e + 2 < E:
                 w1_interleave(2 * e + 2)
                 w1_interleave(2 * e + 3)
             if e == 0:
                 gathers(2)
-            if e == 2:
-                hidden(0)
-        hidden(1)
+        hidden(0)
         w2_prepare(0)
-        w2_prepare(1)
-        layer2(0)
+        hidden(1)
+        w1_interleave(6)
+        w1_interleave(7)
         hidden(2)
+        w1_quantise(6)
+        w1_quantise(7)
+        layer1(3)
+        w2_prepare(1)
         w2_prepare(2)
-        w2_prepare(3)
         hidden(3)
+        layer2(0)
+        w2_prepare(3)
         layer2(1)
         for nt in range(NT):
             combine(nt)

@@ -192,20 +192,22 @@ def tile_routed_moe_kernel(tc, xT, w1, w2, gate, offs, pos1, pos2, out):
                 hs[e] = w2p.tile([P, C], U8, name="hs%d" % e, align_bytes=64, offset=base + C * 4)
             nc.vector.quantize_mx(out=hc[e][:].bitcast(FP8X4), scales=hs[e][:], in_=hg[:].rearrange("p n t -> p (n t)"))
 
-        def w2_prepare(e):
-            wg = grpp.tile([P, NT, P, PACK], BF16, name="w2_grp", tag="grp", align_bytes=64)
-            copy_on(
-                W2_ENGINE[e],
-                wg[:].rearrange("p q (c i) j -> p q c j i", i=4),
-                w2_raw[e][:].rearrange("p j (q c i) -> p q c j i", q=NT, i=4),
-            )
+        def w2_prepare(e, pieces):
             w2c[e] = keep.tile([P, NT, P], U32, name="w2c%d" % e, align_bytes=64)
             w2s[e] = keep.tile([P, NT, P], U8, name="w2s%d" % e, align_bytes=64)
-            nc.vector.quantize_mx(
-                out=w2c[e][:].rearrange("p q c -> p (q c)").bitcast(FP8X4),
-                scales=w2s[e][:].rearrange("p q c -> p (q c)"),
-                in_=wg[:].rearrange("p q c j -> p (q c j)"),
-            )
+            nq = NT // pieces
+            for q0 in range(0, NT, nq):
+                wg = grpp.tile([P, nq, P, PACK], BF16, name="w2_grp", tag="grp", align_bytes=64)
+                copy_on(
+                    W2_ENGINE[e],
+                    wg[:].rearrange("p q (c i) j -> p q c j i", i=4),
+                    w2_raw[e][:, :, q0 * P:(q0 + nq) * P].rearrange("p j (q c i) -> p q c j i", q=nq, i=4),
+                )
+                nc.vector.quantize_mx(
+                    out=w2c[e][:, q0:q0 + nq].rearrange("p q c -> p (q c)").bitcast(FP8X4),
+                    scales=w2s[e][:, q0:q0 + nq].rearrange("p q c -> p (q c)"),
+                    in_=wg[:].rearrange("p q c j -> p (q c j)"),
+                )
 
         def layer2(pair):
             ybanks = [psum.tile([P, 2 * C], F32, name="ybank", tag="bank") for nt in range(NT)]
@@ -253,7 +255,7 @@ def tile_routed_moe_kernel(tc, xT, w1, w2, gate, offs, pos1, pos2, out):
             if e == 0:
                 gathers(2)
         hidden(0)
-        w2_prepare(0)
+        w2_prepare(0, 1)
         hidden(1)
         w1_interleave(6)
         w1_interleave(7)
@@ -261,11 +263,11 @@ def tile_routed_moe_kernel(tc, xT, w1, w2, gate, offs, pos1, pos2, out):
         w1_quantise(6)
         w1_quantise(7)
         layer1(3)
-        w2_prepare(1)
-        w2_prepare(2)
+        w2_prepare(1, 1)
+        w2_prepare(2, 1)
         hidden(3)
         layer2(0)
-        w2_prepare(3)
+        w2_prepare(3, 2)
         layer2(1)
         for nt in range(NT):
             combine(nt)

@@ -25,6 +25,7 @@ W1_S_M = (128, 128, 128, 128, 80, 80, 64, 64)
 X_V_TOK = 320
 W2_ENGINE = "vvvv"
 W2_BYTES = PACK * N * 4
+H_ON_W1 = (4, 5, 7)
 H_ON_W2 = (None, 0, 0, 2)
 GATHER_CUTS = (0, 384, 768, 1024)
 
@@ -177,8 +178,8 @@ def tile_routed_moe_kernel(tc, xT, w1, w2, gate, offs, pos1, pos2, out):
                 banks[(e, hf)] = bank
 
         def hidden(e):
-            if e < 2:
-                hg = rawp.tile([P, C, PACK], BF16, name="hgrp_r", tag="raw%d" % (e + 4), align_bytes=64)
+            if e < 3:
+                hg = rawp.tile([P, C, PACK], BF16, name="hgrp_r", tag="raw%d" % H_ON_W1[e], align_bytes=64)
             else:
                 hg = hgp.tile([P, C, PACK], BF16, name="hgrp", tag="hgrp", align_bytes=64)
             for hf in range(C // P):
@@ -223,8 +224,12 @@ def tile_routed_moe_kernel(tc, xT, w1, w2, gate, offs, pos1, pos2, out):
                         start=True,
                         stop=True,
                     )
-            for nt in range(NT):
-                nc.scalar.copy(out=ysb[nt][:, pair * 2 * C:(pair + 1) * 2 * C], in_=ybanks[nt][:])
+                if pair == 1:
+                    for nt in range(NT):
+                        nc.scalar.copy(out=ysb[nt][:, e * C:(e + 1) * C], in_=ybanks[nt][:, half * C:(half + 1) * C])
+            if pair == 0:
+                for nt in range(NT):
+                    nc.scalar.copy(out=ysb[nt][:, 0:2 * C], in_=ybanks[nt][:])
 
         def combine(nt):
             pr1 = outp.tile([P, T], F32, name="pr1", tag="pr1")

@@ -23,7 +23,10 @@ TH = T // 2
 NH = N // 2
 W1_S_M = (128, 128, 128, 128, 80, 80, 64, 64)
 X_V_TOK = 320
-W2_ENGINE = "vvvv"
+W2_WHOLE = ((0, 0, NT),)
+W2_FIRST = ((1, 0, 2), (2, 0, 2), (3, 0, 2))
+W2_SECOND = ((1, 2, NT), (2, 2, NT), (3, 2, NT))
+W2_ON_SCALAR = ((2, 2, NT), (3, 2, NT))
 W2_BYTES = PACK * N * 4
 H_ON_W1 = (4, 5, 7)
 H_ON_W2 = (None, 0, 0, 2)
@@ -72,7 +75,7 @@ def tile_routed_moe_kernel(tc, xT, w1, w2, gate, offs, pos1, pos2, out):
         nc.scalar.activation(out=warm_out[:], in_=warm_in[:], func=silu)
 
         w1_raw = []
-        w2_raw = []
+        w2_raw = {}
 
         def load_w1(e):
             for g in range(G):
@@ -80,31 +83,38 @@ def tile_routed_moe_kernel(tc, xT, w1, w2, gate, offs, pos1, pos2, out):
                 nc.sync.dma_start(out=wr[:], in_=w1[e, g * K_PASS:(g + 1) * K_PASS, :].rearrange("(p j) c -> p j c", j=PACK))
                 w1_raw.append(wr)
 
-        def load_w2(e):
-            wr = w2p.tile([P, PACK, N], F32, name="w2_raw%d" % e, align_bytes=64, offset=e * W2_BYTES)
-            nc.sync.dma_start(out=wr[:], in_=w2[e].rearrange("(p j) c -> p j c", j=PACK))
-            w2_raw.append(wr)
+        def load_w2(piece):
+            e, q0, q1 = piece
+            wr = w2p.tile([P, PACK, (q1 - q0) * P], F32, name="w2_raw%d_%d" % (e, q0), align_bytes=64, offset=e * W2_BYTES + q0 * PACK * P * 4)
+            nc.sync.dma_start(out=wr[:], in_=w2[e].rearrange("(p j) c -> p j c", j=PACK)[:, :, q0 * P:q1 * P])
+            w2_raw[piece] = wr
+
+        gate_t = {}
+
+        def load_gate(nt):
+            for r in range(2):
+                gt = keep.tile([P, T], F32, name="gate%d_%d" % (r, nt))
+                nc.sync.dma_start(out=gt[:], in_=gate[r, nt * P:(nt + 1) * P, :])
+                gate_t[(r, nt)] = gt
 
         load_w1(0)
         load_w1(1)
         load_w1(2)
-        load_w2(0)
+        load_w2(W2_WHOLE[0])
         load_w1(3)
-        load_w2(1)
-        load_w2(2)
-        load_w2(3)
+        for piece in W2_FIRST:
+            load_w2(piece)
 
         pos1_t = lists.tile([P, T // 16], U16, name="pos1_t")
         nc.sync.dma_start(pos1_t[:], pos1)
         pos2_t = lists.tile([P, T // 16], U16, name="pos2_t")
         nc.sync.dma_start(pos2_t[:], pos2)
-
-        gate_t = {}
-        for nt in range(NT):
-            for r in range(2):
-                gt = keep.tile([P, T], F32, name="gate%d_%d" % (r, nt))
-                nc.sync.dma_start(out=gt[:], in_=gate[r, nt * P:(nt + 1) * P, :])
-                gate_t[(r, nt)] = gt
+        load_w2(W2_SECOND[0])
+        load_w2(W2_SECOND[1])
+        load_gate(0)
+        load_w2(W2_SECOND[2])
+        for nt in range(1, NT):
+            load_gate(nt)
 
         xw = []
         xs = keep.tile([P, T], U8, name="xs", align_bytes=64)
@@ -193,28 +203,30 @@ def tile_routed_moe_kernel(tc, xT, w1, w2, gate, offs, pos1, pos2, out):
                 hs[e] = w2p.tile([P, C], U8, name="hs%d" % e, align_bytes=64, offset=base + C * 4)
             nc.vector.quantize_mx(out=hc[e][:].bitcast(FP8X4), scales=hs[e][:], in_=hg[:].rearrange("p n t -> p (n t)"))
 
-        def w2_prepare(e, pieces):
+        for e in range(E):
             w2c[e] = keep.tile([P, NT, P], U32, name="w2c%d" % e, align_bytes=64)
             w2s[e] = keep.tile([P, NT, P], U8, name="w2s%d" % e, align_bytes=64)
-            nq = NT // pieces
-            for q0 in range(0, NT, nq):
-                wg = grpp.tile([P, nq, P, PACK], BF16, name="w2_grp", tag="grp", align_bytes=64)
-                copy_on(
-                    W2_ENGINE[e],
-                    wg[:].rearrange("p q (c i) j -> p q c j i", i=4),
-                    w2_raw[e][:, :, q0 * P:(q0 + nq) * P].rearrange("p j (q c i) -> p q c j i", q=nq, i=4),
-                )
-                nc.vector.quantize_mx(
-                    out=w2c[e][:, q0:q0 + nq].rearrange("p q c -> p (q c)").bitcast(FP8X4),
-                    scales=w2s[e][:, q0:q0 + nq].rearrange("p q c -> p (q c)"),
-                    in_=wg[:].rearrange("p q c j -> p (q c j)"),
-                )
 
-        def layer2(pair):
-            ybanks = [psum.tile([P, 2 * C], F32, name="ybank", tag="bank") for nt in range(NT)]
+        def w2_prepare(piece):
+            e, q0, q1 = piece
+            nq = q1 - q0
+            wg = grpp.tile([P, nq, P, PACK], BF16, name="w2_grp", tag="grp", align_bytes=64)
+            copy_on(
+                "s" if piece in W2_ON_SCALAR else "v",
+                wg[:].rearrange("p q (c i) j -> p q c j i", i=4),
+                w2_raw[piece][:].rearrange("p j (q c i) -> p q c j i", q=nq, i=4),
+            )
+            nc.vector.quantize_mx(
+                out=w2c[e][:, q0:q1].rearrange("p q c -> p (q c)").bitcast(FP8X4),
+                scales=w2s[e][:, q0:q1].rearrange("p q c -> p (q c)"),
+                in_=wg[:].rearrange("p q c j -> p (q c j)"),
+            )
+
+        def layer2(pair, blocks):
+            ybanks = {nt: psum.tile([P, 2 * C], F32, name="ybank", tag="bank") for nt in blocks}
             for half in range(2):
                 e = 2 * pair + half
-                for nt in range(NT):
+                for nt in blocks:
                     nc.tensor.matmul_mx(
                         out=ybanks[nt][:, half * C:(half + 1) * C],
                         lhsT=w2c[e][:, nt].bitcast(FP8X4),
@@ -225,10 +237,10 @@ def tile_routed_moe_kernel(tc, xT, w1, w2, gate, offs, pos1, pos2, out):
                         stop=True,
                     )
                 if pair == 1:
-                    for nt in range(NT):
+                    for nt in blocks:
                         nc.scalar.copy(out=ysb[nt][:, e * C:(e + 1) * C], in_=ybanks[nt][:, half * C:(half + 1) * C])
             if pair == 0:
-                for nt in range(NT):
+                for nt in blocks:
                     nc.scalar.copy(out=ysb[nt][:, 0:2 * C], in_=ybanks[nt][:])
 
         def combine(nt):
@@ -244,7 +256,8 @@ def tile_routed_moe_kernel(tc, xT, w1, w2, gate, offs, pos1, pos2, out):
                 nc.scalar.copy(out=res[:], in_=acc[:])
             else:
                 nc.vector.tensor_tensor(res[:], pr1[:], pr2[:], add)
-            nc.sync.dma_start(out=out[nt * P:(nt + 1) * P, :], in_=res[:])
+            store = nc.scalar if nt < NT - 1 else nc.sync
+            store.dma_start(out=out[nt * P:(nt + 1) * P, :], in_=res[:])
 
         gathers(0)
         w1_interleave(0)
@@ -260,7 +273,7 @@ def tile_routed_moe_kernel(tc, xT, w1, w2, gate, offs, pos1, pos2, out):
             if e == 0:
                 gathers(2)
         hidden(0)
-        w2_prepare(0, 1)
+        w2_prepare(W2_WHOLE[0])
         hidden(1)
         w1_interleave(6)
         w1_interleave(7)
@@ -268,11 +281,15 @@ def tile_routed_moe_kernel(tc, xT, w1, w2, gate, offs, pos1, pos2, out):
         w1_quantise(6)
         w1_quantise(7)
         layer1(3)
-        w2_prepare(1, 1)
-        w2_prepare(2, 1)
+        w2_prepare(W2_FIRST[0])
+        w2_prepare(W2_FIRST[1])
         hidden(3)
-        layer2(0)
-        w2_prepare(3, 2)
-        layer2(1)
+        layer2(0, (0, 1))
+        w2_prepare(W2_FIRST[2])
+        layer2(1, (0, 1))
+        for piece in W2_SECOND:
+            w2_prepare(piece)
+        layer2(0, (2, 3))
+        layer2(1, (2, 3))
         for nt in range(NT):
             combine(nt)

@@ -1,7 +1,6 @@
 from contextlib import ExitStack
 
 import concourse.mybir as mybir
-from concourse.masks import make_identity
 
 K, T, E, C, H, N = 1024, 512, 4, 256, 512, 512
 FLOPS = 2 * E * C * (K * H + H * N)
@@ -21,15 +20,16 @@ G = K // K_PASS
 NT = N // P
 TH = T // 2
 NH = N // 2
-W1_S_M = (128, 128, 128, 128, 80, 80, 64, 64)
-X_V_TOK = 320
+W1_S_M = (128, 128, 128, 96, 80, 64, 0, 64)
+X_V_TOK = (320, 128)
 W2_WHOLE = ((0, 0, NT),)
 W2_FIRST = ((1, 0, 2), (2, 0, 2), (3, 0, 2))
 W2_SECOND = ((1, 2, NT), (2, 2, NT), (3, 2, NT))
 W2_ON_SCALAR = ((2, 2, NT), (3, 2, NT))
+RAW_BYTES = PACK * H * 4
 W2_BYTES = PACK * N * 4
-H_ON_W1 = (4, 5, 7)
-H_ON_W2 = (None, 0, 0, 2)
+H_ON_W1 = (5, 5, 6)
+H_ON_W2 = (None, None, None, 3)
 GATHER_CUTS = (0, 384, 768, 1024)
 
 
@@ -62,12 +62,9 @@ def tile_routed_moe_kernel(tc, xT, w1, w2, gate, offs, pos1, pos2, out):
 
         x_raw = []
         for g in range(G):
-            xr = rawp.tile([P, PACK, T], F32, name="x_raw", tag="raw%d" % (6 + g), align_bytes=64)
+            xr = rawp.tile([P, PACK, T], F32, name="x_raw%d" % g, align_bytes=64, offset=(6 + g) * RAW_BYTES)
             nc.sync.dma_start(out=xr[:], in_=xT[g * K_PASS:(g + 1) * K_PASS, :].rearrange("(p j) t -> p j t", j=PACK))
             x_raw.append(xr)
-
-        ident = keep.tile([P, P], F32, name="ident")
-        make_identity(nc, ident[:])
 
         warm_in = keep.tile([P, 1], F32, name="warm_in")
         warm_out = keep.tile([P, 1], F32, name="warm_out")
@@ -79,7 +76,7 @@ def tile_routed_moe_kernel(tc, xT, w1, w2, gate, offs, pos1, pos2, out):
 
         def load_w1(e):
             for g in range(G):
-                wr = rawp.tile([P, PACK, H], F32, name="w_raw", tag="raw%d" % (e * G + g), align_bytes=64)
+                wr = rawp.tile([P, PACK, H], F32, name="w_raw%d_%d" % (e, g), align_bytes=64, offset=(e * G + g) * RAW_BYTES)
                 nc.sync.dma_start(out=wr[:], in_=w1[e, g * K_PASS:(g + 1) * K_PASS, :].rearrange("(p j) c -> p j c", j=PACK))
                 w1_raw.append(wr)
 
@@ -100,8 +97,8 @@ def tile_routed_moe_kernel(tc, xT, w1, w2, gate, offs, pos1, pos2, out):
         load_w1(0)
         load_w1(1)
         load_w1(2)
-        load_w2(W2_WHOLE[0])
         load_w1(3)
+        load_w2(W2_WHOLE[0])
         for piece in W2_FIRST:
             load_w2(piece)
 
@@ -124,7 +121,7 @@ def tile_routed_moe_kernel(tc, xT, w1, w2, gate, offs, pos1, pos2, out):
             xw.append(w_)
         for g in range(G):
             xg = grpp.tile([P, T, PACK], BF16, name="x_grp", tag="grp", align_bytes=64)
-            v_tok = X_V_TOK if g == 0 else 0
+            v_tok = X_V_TOK[g]
             for engine, t0, t1 in (("v", 0, v_tok), ("s", v_tok, T)):
                 if t1 == t0:
                     continue
@@ -157,7 +154,8 @@ def tile_routed_moe_kernel(tc, xT, w1, w2, gate, offs, pos1, pos2, out):
             dst = wg[:].rearrange("p t m j -> p m j t")
             src = w1_raw[ci][:].rearrange("p j (m t) -> p m j t", t=PACK)
             s_m = W1_S_M[ci]
-            copy_on("s", dst[:, 0:s_m], src[:, 0:s_m])
+            if s_m > 0:
+                copy_on("s", dst[:, 0:s_m], src[:, 0:s_m])
             if s_m < P:
                 copy_on("v", dst[:, s_m:P], src[:, s_m:P])
             w1g[ci] = wg
@@ -189,12 +187,12 @@ def tile_routed_moe_kernel(tc, xT, w1, w2, gate, offs, pos1, pos2, out):
 
         def hidden(e):
             if e < 3:
-                hg = rawp.tile([P, C, PACK], BF16, name="hgrp_r", tag="raw%d" % H_ON_W1[e], align_bytes=64)
+                hg = rawp.tile([P, C, PACK], BF16, name="hgrp_r%d" % e, align_bytes=64, offset=H_ON_W1[e] * RAW_BYTES + e * C * PACK * 2)
             else:
                 hg = hgp.tile([P, C, PACK], BF16, name="hgrp", tag="hgrp", align_bytes=64)
             for hf in range(C // P):
                 nc.scalar.activation(out=hg[:, hf * P:(hf + 1) * P, :], in_=banks[(e, hf)][:].rearrange("p t n -> p n t"), func=silu)
-            if e == 0:
+            if H_ON_W2[e] is None:
                 hc[e] = keep.tile([P, C], U32, name="hc%d" % e, align_bytes=64)
                 hs[e] = keep.tile([P, C], U8, name="hs%d" % e, align_bytes=64)
             else:
@@ -207,19 +205,23 @@ def tile_routed_moe_kernel(tc, xT, w1, w2, gate, offs, pos1, pos2, out):
             w2c[e] = keep.tile([P, NT, P], U32, name="w2c%d" % e, align_bytes=64)
             w2s[e] = keep.tile([P, NT, P], U8, name="w2s%d" % e, align_bytes=64)
 
-        def w2_prepare(piece):
+        def w2_interleave(piece):
             e, q0, q1 = piece
             nq = q1 - q0
             wg = grpp.tile([P, nq, P, PACK], BF16, name="w2_grp", tag="grp", align_bytes=64)
+            w2g[piece] = wg
             copy_on(
                 "s" if piece in W2_ON_SCALAR else "v",
                 wg[:].rearrange("p q (c i) j -> p q c j i", i=4),
                 w2_raw[piece][:].rearrange("p j (q c i) -> p q c j i", q=nq, i=4),
             )
+
+        def w2_quantise(piece):
+            e, q0, q1 = piece
             nc.vector.quantize_mx(
                 out=w2c[e][:, q0:q1].rearrange("p q c -> p (q c)").bitcast(FP8X4),
                 scales=w2s[e][:, q0:q1].rearrange("p q c -> p (q c)"),
-                in_=wg[:].rearrange("p q c j -> p (q c j)"),
+                in_=w2g[piece][:].rearrange("p q c j -> p (q c j)"),
             )
 
         def layer2(pair, blocks):
@@ -249,15 +251,8 @@ def tile_routed_moe_kernel(tc, xT, w1, w2, gate, offs, pos1, pos2, out):
             res = resp.tile([P, T], F32, name="res", tag="res")
             nc.vector.tensor_tensor(pr1[:], ysb[nt][:].indirect(pos1_t[:]), gate_t[(0, nt)][:], mult)
             nc.vector.tensor_tensor(pr2[:], ysb[nt][:].indirect(pos2_t[:]), gate_t[(1, nt)][:], mult)
-            if nt < NT - 1:
-                acc = psum.tile([P, T], F32, name="obank", tag="bank")
-                nc.tensor.matmul(acc[:], lhsT=ident[:], rhs=pr1[:], start=True, stop=False)
-                nc.tensor.matmul(acc[:], lhsT=ident[:], rhs=pr2[:], start=False, stop=True)
-                nc.scalar.copy(out=res[:], in_=acc[:])
-            else:
-                nc.vector.tensor_tensor(res[:], pr1[:], pr2[:], add)
-            store = nc.scalar if nt < NT - 1 else nc.sync
-            store.dma_start(out=out[nt * P:(nt + 1) * P, :], in_=res[:])
+            nc.vector.tensor_tensor(res[:], pr1[:], pr2[:], add)
+            nc.sync.dma_start(out=out[nt * P:(nt + 1) * P, :], in_=res[:])
 
         gathers(0)
         w1_interleave(0)
@@ -273,23 +268,33 @@ def tile_routed_moe_kernel(tc, xT, w1, w2, gate, offs, pos1, pos2, out):
             if e == 0:
                 gathers(2)
         hidden(0)
-        w2_prepare(W2_WHOLE[0])
-        hidden(1)
         w1_interleave(6)
+        hidden(1)
         w1_interleave(7)
-        hidden(2)
         w1_quantise(6)
+        hidden(2)
         w1_quantise(7)
         layer1(3)
-        w2_prepare(W2_FIRST[0])
-        w2_prepare(W2_FIRST[1])
+        w2_interleave(W2_WHOLE[0])
+        w2_interleave(W2_FIRST[0])
+        w2_quantise(W2_WHOLE[0])
+        w2_interleave(W2_FIRST[1])
+        w2_quantise(W2_FIRST[0])
+        w2_quantise(W2_FIRST[1])
+        w2_interleave(W2_FIRST[2])
         hidden(3)
         layer2(0, (0, 1))
-        w2_prepare(W2_FIRST[2])
+        w2_quantise(W2_FIRST[2])
         layer2(1, (0, 1))
-        for piece in W2_SECOND:
-            w2_prepare(piece)
+        w2_interleave(W2_SECOND[0])
+        w2_interleave(W2_SECOND[1])
+        w2_interleave(W2_SECOND[2])
+        w2_quantise(W2_SECOND[0])
+        w2_quantise(W2_SECOND[1])
+        w2_quantise(W2_SECOND[2])
         layer2(0, (2, 3))
         layer2(1, (2, 3))
-        for nt in range(NT):
-            combine(nt)
+        combine(0)
+        combine(1)
+        combine(2)
+        combine(3)

@@ -205,24 +205,26 @@ def tile_routed_moe_kernel(tc, xT, w1, w2, gate, offs, pos1, pos2, out):
             w2c[e] = keep.tile([P, NT, P], U32, name="w2c%d" % e, align_bytes=64)
             w2s[e] = keep.tile([P, NT, P], U8, name="w2s%d" % e, align_bytes=64)
 
-        def w2_interleave(piece):
+        def w2_interleave(piece, step=NT):
             e, q0, q1 = piece
             nq = q1 - q0
             wg = grpp.tile([P, nq, P, PACK], BF16, name="w2_grp", tag="grp", align_bytes=64)
             w2g[piece] = wg
-            copy_on(
-                "s" if piece in W2_ON_SCALAR else "v",
-                wg[:].rearrange("p q (c i) j -> p q c j i", i=4),
-                w2_raw[piece][:].rearrange("p j (q c i) -> p q c j i", q=nq, i=4),
-            )
+            dst = wg[:].rearrange("p q (c i) j -> p q c j i", i=4)
+            src = w2_raw[piece][:].rearrange("p j (q c i) -> p q c j i", q=nq, i=4)
+            for b0 in range(0, nq, step):
+                b1 = min(b0 + step, nq)
+                copy_on("s" if piece in W2_ON_SCALAR else "v", dst[:, b0:b1], src[:, b0:b1])
 
-        def w2_quantise(piece):
+        def w2_quantise(piece, step=NT):
             e, q0, q1 = piece
-            nc.vector.quantize_mx(
-                out=w2c[e][:, q0:q1].rearrange("p q c -> p (q c)").bitcast(FP8X4),
-                scales=w2s[e][:, q0:q1].rearrange("p q c -> p (q c)"),
-                in_=w2g[piece][:].rearrange("p q c j -> p (q c j)"),
-            )
+            for b0 in range(0, q1 - q0, step):
+                b1 = min(b0 + step, q1 - q0)
+                nc.vector.quantize_mx(
+                    out=w2c[e][:, q0 + b0:q0 + b1].rearrange("p q c -> p (q c)").bitcast(FP8X4),
+                    scales=w2s[e][:, q0 + b0:q0 + b1].rearrange("p q c -> p (q c)"),
+                    in_=w2g[piece][:, b0:b1].rearrange("p q c j -> p (q c j)"),
+                )
 
         def layer2(pair, blocks):
             ybanks = {nt: psum.tile([P, 2 * C], F32, name="ybank", tag="bank") for nt in blocks}
@@ -288,10 +290,10 @@ def tile_routed_moe_kernel(tc, xT, w1, w2, gate, offs, pos1, pos2, out):
         layer2(1, (0, 1))
         w2_interleave(W2_SECOND[0])
         w2_interleave(W2_SECOND[1])
-        w2_interleave(W2_SECOND[2])
+        w2_interleave(W2_SECOND[2], 1)
         w2_quantise(W2_SECOND[0])
         w2_quantise(W2_SECOND[1])
-        w2_quantise(W2_SECOND[2])
+        w2_quantise(W2_SECOND[2], 1)
         layer2(0, (2, 3))
         layer2(1, (2, 3))
         combine(0)

from contextlib import ExitStack

import concourse.mybir as mybir

K, T, E, C, H, N = 1024, 512, 4, 256, 512, 512
FLOPS = 2 * E * C * (K * H + H * N)

F32 = mybir.dt.float32
BF16 = mybir.dt.bfloat16
U32 = mybir.dt.uint32
U16 = mybir.dt.uint16
U8 = mybir.dt.uint8
I32 = mybir.dt.int32
FP8X4 = mybir.dt.float8_e4m3fn_x4

P = 128
PACK = 4
K_PASS = P * PACK
G = K // K_PASS
NT = N // P
TH = T // 2
NH = N // 2
W1_S_M = (128, 128, 128, 96, 80, 64, 0, 64)
X_V_TOK = (320, 128)
W2_WHOLE = ((0, 0, NT),)
W2_FIRST = ((1, 0, 2), (2, 0, 2), (3, 0, 2))
W2_SECOND = ((1, 2, NT), (2, 2, NT), (3, 2, NT))
W2_ON_SCALAR = ((2, 2, NT), (3, 2, NT))
RAW_BYTES = PACK * H * 4
W2_BYTES = PACK * N * 4
H_ON_W1 = (5, 5, 6)
H_ON_W2 = (None, None, None, 3)
GATHER_CUTS = (0, 384, 768, 1024)


def tile_routed_moe_kernel(tc, xT, w1, w2, gate, offs, pos1, pos2, out):
    nc = tc.nc
    silu = mybir.ActivationFunctionType.Silu
    mult = mybir.AluOpType.mult
    add = mybir.AluOpType.add

    def copy_on(engine, dst, src):
        if engine == "v":
            nc.vector.tensor_copy(out=dst, in_=src)
        else:
            nc.scalar.copy(out=dst, in_=src)

    with ExitStack() as ctx:
        lists = ctx.enter_context(tc.tile_pool(name="lists", bufs=1))
        keep = ctx.enter_context(tc.tile_pool(name="keep", bufs=1))
        rawp = ctx.enter_context(tc.tile_pool(name="rawp", bufs=1))
        grpp = ctx.enter_context(tc.tile_pool(name="grpp", bufs=4))
        pinp = ctx.enter_context(tc.tile_pool(name="pinp", bufs=1))
        hgp = ctx.enter_context(tc.tile_pool(name="hgp", bufs=2))
        outp = ctx.enter_context(tc.tile_pool(name="outp", bufs=2))
        w2p = ctx.enter_context(tc.tile_pool(name="w2p", bufs=1))
        resp = ctx.enter_context(tc.tile_pool(name="resp", bufs=NT))
        psum = ctx.enter_context(tc.psum_pool(name="psum", bufs=8))

        offs_t = lists.tile([P, E * C // 16], U16, name="offs_t")
        nc.sync.dma_start(offs_t[:], offs)

        x_raw = []
        for g in range(G):
            xr = rawp.tile([P, PACK, T], F32, name="x_raw%d" % g, align_bytes=64, offset=(6 + g) * RAW_BYTES)
            nc.sync.dma_start(out=xr[:], in_=xT[g * K_PASS:(g + 1) * K_PASS, :].rearrange("(p j) t -> p j t", j=PACK))
            x_raw.append(xr)

        warm_in = keep.tile([P, 1], F32, name="warm_in")
        warm_out = keep.tile([P, 1], F32, name="warm_out")
        nc.vector.memset(warm_in[:], 0.0)
        nc.scalar.activation(out=warm_out[:], in_=warm_in[:], func=silu)

        w1_raw = []
        w2_raw = {}

        def load_w1(e):
            for g in range(G):
                wr = rawp.tile([P, PACK, H], F32, name="w_raw%d_%d" % (e, g), align_bytes=64, offset=(e * G + g) * RAW_BYTES)
                nc.sync.dma_start(out=wr[:], in_=w1[e, g * K_PASS:(g + 1) * K_PASS, :].rearrange("(p j) c -> p j c", j=PACK))
                w1_raw.append(wr)

        def load_w2(piece):
            e, q0, q1 = piece
            wr = w2p.tile([P, PACK, (q1 - q0) * P], F32, name="w2_raw%d_%d" % (e, q0), align_bytes=64, offset=e * W2_BYTES + q0 * PACK * P * 4)
            nc.sync.dma_start(out=wr[:], in_=w2[e].rearrange("(p j) c -> p j c", j=PACK)[:, :, q0 * P:q1 * P])
            w2_raw[piece] = wr

        gate_t = {}

        def load_gate(nt):
            for r in range(2):
                gt = keep.tile([P, T], F32, name="gate%d_%d" % (r, nt))
                nc.sync.dma_start(out=gt[:], in_=gate[r, nt * P:(nt + 1) * P, :])
                gate_t[(r, nt)] = gt

        load_w1(0)
        load_w1(1)
        load_w1(2)
        load_w1(3)
        load_w2(W2_WHOLE[0])
        for piece in W2_FIRST:
            load_w2(piece)

        pos1_t = lists.tile([P, T // 16], U16, name="pos1_t")
        nc.sync.dma_start(pos1_t[:], pos1)
        pos2_t = lists.tile([P, T // 16], U16, name="pos2_t")
        nc.sync.dma_start(pos2_t[:], pos2)
        load_w2(W2_SECOND[0])
        load_w2(W2_SECOND[1])
        load_gate(0)
        load_w2(W2_SECOND[2])
        for nt in range(1, NT):
            load_gate(nt)

        xw = []
        xs = keep.tile([P, T], U8, name="xs", align_bytes=64)
        nc.vector.memset(xs[:].bitcast(I32), 0)
        for g in range(G):
            w_ = keep.tile([P, T], U32, name="xw%d" % g, align_bytes=64)
            xw.append(w_)
        for g in range(G):
            xg = grpp.tile([P, T, PACK], BF16, name="x_grp", tag="grp", align_bytes=64)
            v_tok = X_V_TOK[g]
            for engine, t0, t1 in (("v", 0, v_tok), ("s", v_tok, T)):
                if t1 == t0:
                    continue
                copy_on(
                    engine,
                    xg[:, t0:t1, :].rearrange("p (c i) j -> p c j i", i=4),
                    x_raw[g][:, :, t0:t1].rearrange("p j (c i) -> p c j i", i=4),
                )
            nc.vector.quantize_mx(out=xw[g][:].bitcast(FP8X4), scales=xs[PACK * g:P, :], in_=xg[:].rearrange("p t j -> p (t j)"))

        ysb = [keep.tile([P, E * C], F32, name="ysb%d" % nt) for nt in range(NT)]
        xgw, xgs, w1g, w1c, w1s, banks, hgs, hc, hs = {}, {}, {}, {}, {}, {}, {}, {}, {}
        w2g, w2c, w2s = {}, {}, {}

        def gathers(k):
            a, b = GATHER_CUTS[k], GATHER_CUTS[k + 1]
            lst = offs_t[:, a // 16:b // 16]
            tags = ("xgw%d" % k, "xgs%d" % k) if k < 2 else ("pin0", "pin1")
            xgw[k] = pinp.tile([P, G, b - a], U32, name="xgw", tag=tags[0], align_bytes=64)
            xgs[k] = pinp.tile([P, b - a], U8, name="xgs", tag=tags[1], align_bytes=64)
            for g in range(G):
                nc.vector.tensor_copy(out=xgw[k][:, g, :], in_=xw[g][:].indirect(lst))
            nc.vector.tensor_copy(out=xgs[k][:], in_=xs[:].indirect(lst))

        def w1_interleave(ci):
            if ci < 2:
                wg = pinp.tile([P, PACK, P, PACK], BF16, name="w1_grp_p", tag="pin%d" % ci, align_bytes=64)
            else:
                wg = grpp.tile([P, PACK, P, PACK], BF16, name="w1_grp", tag="grp", align_bytes=64)
            dst = wg[:].rearrange("p t m j -> p m j t")
            src = w1_raw[ci][:].rearrange("p j (m t) -> p m j t", t=PACK)
            s_m = W1_S_M[ci]
            if s_m > 0:
                copy_on("s", dst[:, 0:s_m], src[:, 0:s_m])
            if s_m < P:
                copy_on("v", dst[:, s_m:P], src[:, s_m:P])
            w1g[ci] = wg

        def w1_quantise(ci):
            w1c[ci] = keep.tile([P, H], U32, name="w1c%d" % ci, align_bytes=64)
            w1s[ci] = keep.tile([P, H], U8, name="w1s%d" % ci, align_bytes=64)
            nc.vector.quantize_mx(out=w1c[ci][:].bitcast(FP8X4), scales=w1s[ci][:], in_=w1g[ci][:].rearrange("p t m j -> p (t m j)"))

        def layer1(e):
            for hf in range(C // P):
                bank = psum.tile([P, PACK, P], F32, name="abank", tag="bank")
                slot0 = e * C + hf * P
                k = max(i for i in range(3) if GATHER_CUTS[i] <= slot0)
                cols = slice(slot0 - GATHER_CUTS[k], slot0 - GATHER_CUTS[k] + P)
                for t in range(PACK):
                    m_cols = slice(t * P, (t + 1) * P)
                    for g in range(G):
                        nc.tensor.matmul_mx(
                            out=bank[:, t, :],
                            lhsT=w1c[e * G + g][:, m_cols].bitcast(FP8X4),
                            lhsT_scale=w1s[e * G + g][:, m_cols],
                            rhs=xgw[k][:, g, cols].bitcast(FP8X4),
                            rhs_scale=xgs[k][PACK * g:P, cols],
                            start=(g == 0),
                            stop=(g == G - 1),
                        )
                banks[(e, hf)] = bank

        def hidden(e):
            if e < 3:
                hg = rawp.tile([P, C, PACK], BF16, name="hgrp_r%d" % e, align_bytes=64, offset=H_ON_W1[e] * RAW_BYTES + e * C * PACK * 2)
            else:
                hg = hgp.tile([P, C, PACK], BF16, name="hgrp", tag="hgrp", align_bytes=64)
            for hf in range(C // P):
                nc.scalar.activation(out=hg[:, hf * P:(hf + 1) * P, :], in_=banks[(e, hf)][:].rearrange("p t n -> p n t"), func=silu)
            if H_ON_W2[e] is None:
                hc[e] = keep.tile([P, C], U32, name="hc%d" % e, align_bytes=64)
                hs[e] = keep.tile([P, C], U8, name="hs%d" % e, align_bytes=64)
            else:
                base = H_ON_W2[e] * W2_BYTES + (e % 2) * 2 * C * 4
                hc[e] = w2p.tile([P, C], U32, name="hc%d" % e, align_bytes=64, offset=base)
                hs[e] = w2p.tile([P, C], U8, name="hs%d" % e, align_bytes=64, offset=base + C * 4)
            nc.vector.quantize_mx(out=hc[e][:].bitcast(FP8X4), scales=hs[e][:], in_=hg[:].rearrange("p n t -> p (n t)"))

        for e in range(E):
            w2c[e] = keep.tile([P, NT, P], U32, name="w2c%d" % e, align_bytes=64)
            w2s[e] = keep.tile([P, NT, P], U8, name="w2s%d" % e, align_bytes=64)

        def w2_interleave(piece, step=NT):
            e, q0, q1 = piece
            nq = q1 - q0
            wg = grpp.tile([P, nq, P, PACK], BF16, name="w2_grp", tag="grp", align_bytes=64)
            w2g[piece] = wg
            dst = wg[:].rearrange("p q (c i) j -> p q c j i", i=4)
            src = w2_raw[piece][:].rearrange("p j (q c i) -> p q c j i", q=nq, i=4)
            for b0 in range(0, nq, step):
                b1 = min(b0 + step, nq)
                copy_on("s" if piece in W2_ON_SCALAR else "v", dst[:, b0:b1], src[:, b0:b1])

        def w2_quantise(piece, step=NT):
            e, q0, q1 = piece
            for b0 in range(0, q1 - q0, step):
                b1 = min(b0 + step, q1 - q0)
                nc.vector.quantize_mx(
                    out=w2c[e][:, q0 + b0:q0 + b1].rearrange("p q c -> p (q c)").bitcast(FP8X4),
                    scales=w2s[e][:, q0 + b0:q0 + b1].rearrange("p q c -> p (q c)"),
                    in_=w2g[piece][:, b0:b1].rearrange("p q c j -> p (q c j)"),
                )

        def layer2(pair, blocks):
            ybanks = {nt: psum.tile([P, 2 * C], F32, name="ybank", tag="bank") for nt in blocks}
            for half in range(2):
                e = 2 * pair + half
                for nt in blocks:
                    nc.tensor.matmul_mx(
                        out=ybanks[nt][:, half * C:(half + 1) * C],
                        lhsT=w2c[e][:, nt].bitcast(FP8X4),
                        lhsT_scale=w2s[e][:, nt],
                        rhs=hc[e][:].bitcast(FP8X4),
                        rhs_scale=hs[e][:],
                        start=True,
                        stop=True,
                    )
                if pair == 1:
                    for nt in blocks:
                        nc.scalar.copy(out=ysb[nt][:, e * C:(e + 1) * C], in_=ybanks[nt][:, half * C:(half + 1) * C])
            if pair == 0:
                for nt in blocks:
                    nc.scalar.copy(out=ysb[nt][:, 0:2 * C], in_=ybanks[nt][:])

        def combine(nt):
            pr1 = outp.tile([P, T], F32, name="pr1", tag="pr1")
            pr2 = outp.tile([P, T], F32, name="pr2", tag="pr2")
            res = resp.tile([P, T], F32, name="res", tag="res")
            nc.vector.tensor_tensor(pr1[:], ysb[nt][:].indirect(pos1_t[:]), gate_t[(0, nt)][:], mult)
            nc.vector.tensor_tensor(pr2[:], ysb[nt][:].indirect(pos2_t[:]), gate_t[(1, nt)][:], mult)
            nc.vector.tensor_tensor(res[:], pr1[:], pr2[:], add)
            nc.sync.dma_start(out=out[nt * P:(nt + 1) * P, :], in_=res[:])

        gathers(0)
        w1_interleave(0)
        w1_interleave(1)
        gathers(1)
        for e in range(E - 1):
            w1_quantise(2 * e)
            w1_quantise(2 * e + 1)
            layer1(e)
            if e + 2 < E:
                w1_interleave(2 * e + 2)
                w1_interleave(2 * e + 3)
            if e == 0:
                gathers(2)
        hidden(0)
        w1_interleave(6)
        hidden(1)
        w1_interleave(7)
        w1_quantise(6)
        hidden(2)
        w1_quantise(7)
        layer1(3)
        w2_interleave(W2_WHOLE[0])
        w2_interleave(W2_FIRST[0])
        w2_quantise(W2_WHOLE[0])
        w2_interleave(W2_FIRST[1])
        w2_quantise(W2_FIRST[0])
        w2_quantise(W2_FIRST[1])
        w2_interleave(W2_FIRST[2])
        hidden(3)
        layer2(0, (0, 1))
        w2_quantise(W2_FIRST[2])
        layer2(1, (0, 1))
        w2_interleave(W2_SECOND[0])
        w2_interleave(W2_SECOND[1])
        w2_interleave(W2_SECOND[2], 1)
        w2_quantise(W2_SECOND[0])
        w2_quantise(W2_SECOND[1])
        w2_quantise(W2_SECOND[2], 1)
        layer2(0, (2, 3))
        layer2(1, (2, 3))
        combine(0)
        combine(1)
        combine(2)
        combine(3)
